import numpy as np
import ml_dtypes


def mxq(x, axis, fmt="e4m3"):
    dtype, down = {"e4m3": (ml_dtypes.float8_e4m3fn, 7), "e5m2": (ml_dtypes.float8_e5m2, 14)}[fmt]
    v = np.moveaxis(np.asarray(x, np.float32).astype(ml_dtypes.bfloat16).astype(np.float64), axis, -1)
    blocks = v.reshape(v.shape[:-1] + (-1, 32))
    amax = np.abs(blocks).max(-1, keepdims=True)
    byte = np.maximum(np.where(amax > 0, np.frexp(amax)[1] - 1 + 127, 0) - down, 1)
    scale = np.exp2(byte - 127.0)
    codes = (blocks / scale).astype(np.float32).astype(dtype).astype(np.float64)
    return np.moveaxis((codes * scale).reshape(v.shape), -1, axis)


WIDE = False


def mx_kscale(k):
    if not WIDE:
        return np.ones(k)
    levels = np.array([10, -10, 5, -5, 0])
    if k % 512:
        return np.exp2(np.random.permutation(np.resize(levels, k // 32))).repeat(32)
    a = np.empty((k // 512, 16))
    for p in range(k // 512):
        a[p, :8] = np.random.permutation(np.resize(levels, 8))
        for g in range(8):
            far = levels[np.abs(levels - a[p, g]) >= 10]
            a[p, g + 8] = far[np.random.randint(len(far))]
    return np.exp2(a.ravel()).repeat(32)


def f64(x):
    return np.asarray(x).astype(np.float64)


def striped8(idx):
    return np.asarray(idx).reshape(8, -1, 16).transpose(0, 2, 1).reshape(128, -1).astype(np.uint16)


def unstriped8(offs):
    return offs.reshape(8, 16, -1).transpose(0, 2, 1).reshape(8, -1).astype(np.int64)


def pick8(x, idx, run):
    r = np.arange(len(x))
    return x[r[:, None], idx[r % (8 * run) // run]]


E2M1 = np.array([0.0, 0.5, 1.0, 1.5, 2.0, 3.0, 4.0, 6.0, -0.0, -0.5, -1.0, -1.5, -2.0, -3.0, -4.0, -6.0])


def pack_weight(w, fmt):
    k, n = w.shape
    w = f64(np.asarray(w, np.float32).astype(ml_dtypes.bfloat16)).reshape(k // 32, 32, n)
    amax = np.abs(w).max(1)
    if fmt == "e4m3":
        byte = np.frexp(amax)[1] - 1 + 127 - 7
    else:
        mant, ex = np.frexp(amax / 6.0)
        byte = np.where(mant > 0.5, ex, ex - 1) + 127
    byte = np.clip(np.where(amax > 0, byte, 1), 1, 254)
    scaled = (w * np.exp2(127.0 - byte)[:, None, :]).reshape(k, n).astype(np.float32)
    by_word = np.ascontiguousarray(scaled.reshape(k // 512, 128, 4, n).transpose(0, 1, 3, 2))
    if fmt == "e4m3":
        words = by_word.astype(ml_dtypes.float8_e4m3fn).view(np.uint8)
    else:
        c = by_word.astype(ml_dtypes.float4_e2m1fn).view(np.uint8) & 0xF
        words = (c[..., 0::2] | (c[..., 1::2] << 4)).reshape(k // 512, 128, 2 * n)
    return np.ascontiguousarray(words), np.ascontiguousarray(byte.astype(np.uint8).reshape(k // 512, 16, n))


def unpack_weight(words, scales, fmt):
    g, _, n = scales.shape
    words = np.ascontiguousarray(words).reshape(g, 128, n, -1)
    if fmt == "e4m3":
        vals = words.view(ml_dtypes.float8_e4m3fn).astype(np.float64)
    else:
        nib = np.empty((g, 128, n, 4), np.uint8)
        nib[..., 0::2] = words & 0xF
        nib[..., 1::2] = words >> 4
        vals = E2M1[nib]
    vals = vals * np.repeat(np.exp2(scales.astype(np.float64) - 127.0), 8, axis=1)[..., None]
    return vals.transpose(0, 1, 3, 2).reshape(g * 512, n)


def sigmoid(v):
    return 1.0 / (1.0 + np.exp(-v))


D, T, I, Q, E = 512, 1024, 512, 512, 256


def setup_inputs():
    n = np.random.standard_normal
    idx = np.stack([np.random.permutation(T)[:I] for _ in range(8)])
    idx2 = np.stack([np.random.permutation(T)[:I] for _ in range(8)])
    idx3 = np.stack([np.random.permutation(T)[:I] for _ in range(8)])
    idx4 = np.stack([np.random.permutation(T)[:I] for _ in range(8)])
    fd = mx_kscale(D)
    fq = mx_kscale(Q)
    keysp = pack_weight(n((D, T)) / fd[:, None], "e2m1")
    mixp = pack_weight(n((Q, E)) * 1.0 / np.sqrt(Q) / fq[:, None], "e4m3")
    return {
        "query": (n((D, Q)) * 1.0 / np.sqrt(D) * fd[:, None]).astype(np.float32),
        "keys_words": keysp[0],
        "keys_scales": keysp[1],
        "thr": (np.random.uniform(-0.6, 0.6, (Q, 1))).astype(np.float32),
        "slope": (np.random.uniform(1.0, 3.0, (Q, 1))).astype(np.float32),
        "rowf": (np.random.uniform(0.5, 2.0, (Q, 1)) * fq[:, None]).astype(np.float32),
        "mix_words": mixp[0],
        "mix_scales": mixp[1],
        "offs": striped8(idx),
        "offs2": striped8(idx2),
        "offs3": striped8(idx3),
        "offs4": striped8(idx4),
    }


def reference(query, keys_words, keys_scales, thr, slope, rowf, mix_words, mix_scales, offs, offs2, offs3, offs4):
    idx = unstriped8(offs)
    idx2 = unstriped8(offs2)
    idx3 = unstriped8(offs3)
    idx4 = unstriped8(offs4)
    keysu = unpack_weight(keys_words, keys_scales, "e2m1")
    mixu = unpack_weight(mix_words, mix_scales, "e4m3")
    queryq = mxq(f64(query), 0, "e4m3")
    a = queryq.T @ keysu
    s1 = sigmoid(pick8(a, idx, 64) * f64(slope) + f64(thr))
    f1 = np.zeros((Q, T))
    f1[np.arange(Q)[:, None], idx2[np.arange(Q) % 512 // 64]] = s1
    f2 = np.zeros((Q, T))
    f2[np.arange(Q)[:, None], idx3[np.arange(Q) % 512 // 64]] = s1
    r = f1 - f2
    cc = a + r * 2.0
    g = np.maximum(pick8(cc, idx4, 64), pick8(cc, idx2, 64))
    gw = g * f64(rowf)
    gwq = mxq(gw, 0, "e4m3")
    y = mixu.T @ gwq
    return y

@@ -1,0 +1,214 @@
+from contextlib import ExitStack
+
+import concourse.mybir as mybir
+
+D, T, I, Q, E = 512, 1024, 512, 512, 256
+FLOPS = 2 * D * Q * T + 2 * Q * E * I
+
+F32 = mybir.dt.float32
+BF16 = mybir.dt.bfloat16
+I32 = mybir.dt.int32
+U32 = mybir.dt.uint32
+U16 = mybir.dt.uint16
+U8 = mybir.dt.uint8
+FP8X4 = mybir.dt.float8_e4m3fn_x4
+FP4X4 = mybir.dt.float4_e2m1fn_x4
+ALU = mybir.AluOpType
+ACT = mybir.ActivationFunctionType
+
+P = 128
+PACK = 4
+BANK = 512
+HALF = I // 2
+LIST_COLS = I // 16
+
+
+def tile_attend_lenders_one_mixed_kernel(tc, query, keys_words, keys_scales, thr, slope, rowf,
+                                          mix_words, mix_scales, offs, offs2, offs3, offs4, out):
+    nc = tc.nc
+    with ExitStack() as ctx:
+        lists = ctx.enter_context(tc.tile_pool(name="lists", bufs=1))
+        keep = ctx.enter_context(tc.tile_pool(name="keep", bufs=1))
+        ring = ctx.enter_context(tc.tile_pool(name="ring", bufs=2))
+        psum_a = ctx.enter_context(tc.psum_pool(name="psum_a", bufs=4))
+        psum_y = ctx.enter_context(tc.psum_pool(name="psum_y", bufs=4))
+
+        def load_scale_rows(queue, plane, rows):
+            for quad in range(4):
+                queue.dma_start(out=plane[32 * quad : 32 * quad + 4, :].bitcast(I32),
+                                in_=rows[0, 4 * quad : 4 * quad + 4, :].bitcast(I32))
+
+        def load_list(name, source):
+            tile = lists.tile([P, LIST_COLS], U16, name=name)
+            nc.sync.dma_start(tile[:], source)
+            return tile
+
+        def load_row_values(queue, name, source):
+            tile = keep.tile([P, PACK], F32, name=name)
+            queue.dma_start(out=tile[:], in_=source.rearrange("(p t) o -> p (t o)", t=PACK))
+            return tile
+
+        key_plane = keep.tile([P, T], U8, align_bytes=64)
+        nc.vector.memset(key_plane[:].bitcast(I32), 0)
+        q_raw = keep.tile([P, PACK, Q], F32)
+        nc.sync.dma_start(out=q_raw[:], in_=query.rearrange("(p j) q -> p j q", j=PACK))
+        load_scale_rows(nc.scalar, key_plane, keys_scales)
+        key_words = keep.tile([P, 2 * T], U8, align_bytes=64)
+        nc.sync.dma_start(out=key_words[:].bitcast(I32), in_=keys_words[0].bitcast(I32))
+        slope_t = load_row_values(nc.gpsimd, "slope_t", slope)
+        thr_t = load_row_values(nc.gpsimd, "thr_t", thr)
+        gate_list = load_list("gate_list", offs)
+        to_list = load_list("to_list", offs2)
+        from_list = load_list("from_list", offs3)
+        pick_list = load_list("pick_list", offs4)
+
+        lent_to = keep.tile([P, T], F32)
+        lent_from = keep.tile([P, T], F32)
+        nc.vector.memset(lent_to[:], 0.0)
+        nc.vector.memset(lent_from[:], 0.0)
+
+        mix_plane = keep.tile([P, E], U8, align_bytes=64)
+        nc.vector.memset(mix_plane[:].bitcast(I32), 0)
+        rowf_t = load_row_values(nc.gpsimd, "rowf_t", rowf)
+        mix_codes = keep.tile([P, E], U32, align_bytes=64)
+        nc.gpsimd.dma_start(out=mix_codes[:].bitcast(I32),
+                            in_=mix_words[0].rearrange("p e r -> p (e r)").bitcast(I32))
+        load_scale_rows(nc.sync, mix_plane, mix_scales)
+
+        q_bf16 = keep.tile([P, 2, P, PACK], BF16, align_bytes=64)
+        q_operands = []
+
+        def quantise_queries(t0, count):
+            codes = keep.tile([P, count * P], U32, name="q_codes%d" % t0, align_bytes=64)
+            plane = keep.tile([P, count * P], U8, name="q_plane%d" % t0, align_bytes=64)
+            nc.vector.quantize_mx(out=codes[:].bitcast(FP8X4), scales=plane[:],
+                                  in_=q_bf16[:, 0:count].rearrange("p t m j -> p (t m j)"))
+            for k in range(count):
+                q_operands.append((codes[:, k * P : (k + 1) * P], plane[:, k * P : (k + 1) * P]))
+
+        def deal_queries(t0, count):
+            nc.vector.tensor_copy(out=q_bf16[:, 0:count].rearrange("p t m j -> p m j t"),
+                                  in_=q_raw[:].rearrange("p j (m t) -> p m j t", t=PACK)[:, :, :, t0 : t0 + count])
+
+        gw = [keep.tile([P, HALF, PACK], BF16, name="gw%d" % h, align_bytes=64) for h in range(2)]
+        g = keep.tile([P, I], F32)
+        scores = []
+        gates = []
+
+        def slots(h):
+            return slice(h * HALF, (h + 1) * HALF)
+
+        def list_cols(h):
+            return slice(h * LIST_COLS // 2, (h + 1) * LIST_COLS // 2)
+
+        def score(t):
+            codes, plane = q_operands[t]
+            a = keep.tile([P, T], F32, name="a%d" % t)
+            for n in range(T // BANK):
+                cols = slice(n * BANK, (n + 1) * BANK)
+                acc = psum_a.tile([P, BANK], F32, name="acc")
+                nc.tensor.matmul_mx(out=acc[:], lhsT=codes.bitcast(FP8X4), lhsT_scale=plane,
+                                    rhs=key_words[:, 2 * n * BANK : 2 * (n + 1) * BANK].bitcast(FP4X4),
+                                    rhs_scale=key_plane[:, cols], start=True, stop=True)
+                if t == 0:
+                    nc.vector.tensor_copy(out=a[:, cols], in_=acc[:])
+                else:
+                    nc.scalar.copy(out=a[:, cols], in_=acc[:])
+            scores.append(a)
+
+        def gate(t, s1, a, offsets):
+            nc.scalar.activation(out=s1, in_=a[:].indirect(offsets), func=ACT.Sigmoid,
+                                 bias=thr_t[:, t : t + 1], scale=slope_t[:, t : t + 1])
+
+        def double(t, s1):
+            twice = keep.tile([P, I], F32, name="twice%d" % t)
+            nc.scalar.activation(out=twice[:], in_=s1[:], func=ACT.Copy, scale=2.0)
+            gates.append(twice)
+
+        def lend_first():
+            s1 = ring.tile([P, I], F32, name="s1")
+            for h in range(2):
+                half = s1[:, slots(h)]
+                gate(0, half, scores[0], gate_list[:, list_cols(h)])
+                nc.vector.tensor_tensor(out=lent_to[:].indirect(to_list[:, list_cols(h)]), in0=half, in1=half, op=ALU.add)
+            double(0, s1)
+            nc.vector.tensor_copy(out=lent_from[:].indirect(from_list[:]), in_=gates[0][:])
+
+        def lend(t):
+            nc.vector.tensor_copy(out=lent_to[:].indirect(to_list[:]), in_=gates[t][:])
+            nc.vector.tensor_copy(out=lent_from[:].indirect(from_list[:]), in_=gates[t][:])
+
+        def doubled_gate(t):
+            s1 = ring.tile([P, I], F32, name="s1")
+            gate(t, s1[:], scores[t], gate_list[:])
+            double(t, s1)
+
+        def balance(t, engine):
+            part = ring.tile([P, T], F32, name="part")
+            nc.gpsimd.tensor_tensor(out=part[:], in0=scores[t][:], in1=lent_to[:], op=ALU.add)
+            cc = ring.tile([P, T], F32, name="cc")
+            engine.tensor_tensor(out=cc[:], in0=part[:], in1=lent_from[:], op=ALU.subtract)
+            return cc
+
+        def weigh(t, h, larger):
+            nc.scalar.activation(out=gw[h][:, :, t], in_=larger, func=ACT.Copy, scale=rowf_t[:, t : t + 1])
+
+        def pick(t, cc):
+            c4 = ring.tile([P, I], F32, name="c4")
+            c2 = ring.tile([P, I], F32, name="c2")
+            nc.scalar.activation(out=c4[:], in_=cc[:].indirect(pick_list[:]), func=ACT.Copy)
+            nc.scalar.activation(out=c2[:], in_=cc[:].indirect(to_list[:]), func=ACT.Copy)
+            nc.vector.tensor_tensor(out=g[:], in0=c4[:], in1=c2[:], op=ALU.max)
+            for h in range(2):
+                weigh(t, h, g[:, slots(h)])
+
+        def pick_last(t, cc, h):
+            c4 = ring.tile([P, HALF], F32, name="c4_last")
+            c2 = ring.tile([P, HALF], F32, name="c2_last")
+            nc.scalar.activation(out=c4[:], in_=cc[:].indirect(pick_list[:, list_cols(h)]), func=ACT.Copy)
+            nc.vector.tensor_copy(out=c2[:], in_=cc[:].indirect(to_list[:, list_cols(h)]))
+            nc.vector.tensor_tensor(out=g[:, slots(h)], in0=c4[:], in1=c2[:], op=ALU.max)
+            if h == 0:
+                nc.vector.tensor_scalar(out=gw[h][:, :, t], in0=g[:, slots(h)], scalar1=rowf_t[:, t : t + 1], scalar2=None, op0=ALU.mult)
+            else:
+                weigh(t, h, g[:, slots(h)])
+
+        def mix(h):
+            codes = ring.tile([P, HALF], U32, name="gw_codes", align_bytes=64)
+            plane = ring.tile([P, HALF], U8, name="gw_plane", align_bytes=64)
+            nc.vector.quantize_mx(out=codes[:].bitcast(FP8X4), scales=plane[:],
+                                  in_=gw[h][:].rearrange("p i t -> p (i t)"))
+            for e in range(E // P):
+                cols = slice(e * P, (e + 1) * P)
+                y = psum_y.tile([P, HALF], F32, name="y")
+                nc.tensor.matmul_mx(out=y[:], lhsT=mix_codes[:, cols].bitcast(FP8X4), lhsT_scale=mix_plane[:, cols],
+                                    rhs=codes[:].bitcast(FP8X4), rhs_scale=plane[:], start=True, stop=True)
+                y_out = keep.tile([P, HALF], F32, name="y_out%d_%d" % (h, e))
+                if e == 0:
+                    nc.vector.tensor_copy(out=y_out[:], in_=y[:])
+                    nc.sync.dma_start(out=out[cols, slots(h)], in_=y_out[:])
+                else:
+                    nc.scalar.copy(out=y_out[:], in_=y[:])
+                    nc.scalar.dma_start(out=out[cols, slots(h)], in_=y_out[:])
+
+        deal_queries(0, 1)
+        quantise_queries(0, 1)
+        deal_queries(1, 2)
+        score(0)
+        quantise_queries(1, 2)
+        deal_queries(3, 1)
+        quantise_queries(3, 1)
+        lend_first()
+        for t in range(1, PACK):
+            score(t)
+            doubled_gate(t)
+        last = PACK - 1
+        for t in range(last):
+            cc = balance(t, nc.gpsimd)
+            lend(t + 1)
+            pick(t, cc)
+        cc = balance(last, nc.vector)
+        for h in range(2):
+            pick_last(last, cc, h)
+        for h in range(2):
+            mix(h)

@@ -1,6 +1,7 @@
 from contextlib import ExitStack
 
 import concourse.mybir as mybir
+from concourse.masks import make_identity
 
 D, T, I, Q, E = 512, 1024, 512, 512, 256
 FLOPS = 2 * D * Q * T + 2 * Q * E * I
@@ -30,8 +31,7 @@ def tile_attend_lenders_one_mixed_kernel(tc, query, keys_words, keys_scales, thr
         lists = ctx.enter_context(tc.tile_pool(name="lists", bufs=1))
         keep = ctx.enter_context(tc.tile_pool(name="keep", bufs=1))
         ring = ctx.enter_context(tc.tile_pool(name="ring", bufs=2))
-        psum_a = ctx.enter_context(tc.psum_pool(name="psum_a", bufs=4))
-        psum_y = ctx.enter_context(tc.psum_pool(name="psum_y", bufs=4))
+        psum = ctx.enter_context(tc.psum_pool(name="psum", bufs=1))
 
         def load_scale_rows(queue, plane, rows):
             for quad in range(4):
@@ -49,7 +49,7 @@ def tile_attend_lenders_one_mixed_kernel(tc, query, keys_words, keys_scales, thr
             return tile
 
         key_plane = keep.tile([P, T], U8, align_bytes=64)
-        nc.vector.memset(key_plane[:].bitcast(I32), 0)
+        nc.gpsimd.memset(key_plane[:].bitcast(I32), 0)
         q_raw = keep.tile([P, PACK, Q], F32)
         nc.sync.dma_start(out=q_raw[:], in_=query.rearrange("(p j) q -> p j q", j=PACK))
         load_scale_rows(nc.scalar, key_plane, keys_scales)
@@ -66,13 +66,17 @@ def tile_attend_lenders_one_mixed_kernel(tc, query, keys_words, keys_scales, thr
         lent_from = keep.tile([P, T], F32)
         nc.vector.memset(lent_to[:], 0.0)
         nc.vector.memset(lent_from[:], 0.0)
+        minus_two = keep.tile([P, I], F32)
+        nc.vector.memset(minus_two[:], -2.0)
+        identity = keep.tile([P, P], F32)
+        make_identity(nc, identity[:])
 
         mix_plane = keep.tile([P, E], U8, align_bytes=64)
         nc.vector.memset(mix_plane[:].bitcast(I32), 0)
-        rowf_t = load_row_values(nc.gpsimd, "rowf_t", rowf)
+        rowf_t = load_row_values(nc.sync, "rowf_t", rowf)
         mix_codes = keep.tile([P, E], U32, align_bytes=64)
-        nc.gpsimd.dma_start(out=mix_codes[:].bitcast(I32),
-                            in_=mix_words[0].rearrange("p e r -> p (e r)").bitcast(I32))
+        nc.sync.dma_start(out=mix_codes[:].bitcast(I32),
+                          in_=mix_words[0].rearrange("p e r -> p (e r)").bitcast(I32))
         load_scale_rows(nc.sync, mix_plane, mix_scales)
 
         q_bf16 = keep.tile([P, 2, P, PACK], BF16, align_bytes=64)
@@ -91,7 +95,9 @@ def tile_attend_lenders_one_mixed_kernel(tc, query, keys_words, keys_scales, thr
                                   in_=q_raw[:].rearrange("p j (m t) -> p m j t", t=PACK)[:, :, :, t0 : t0 + count])
 
         gw = [keep.tile([P, HALF, PACK], BF16, name="gw%d" % h, align_bytes=64) for h in range(2)]
-        g = keep.tile([P, I], F32)
+        pairs = keep.tile([P, 2, I, 2], BF16)
+        pairs_words = pairs[:].rearrange("p u i e -> p u (i e)").bitcast(U32)
+        larger = [keep.tile([P, I], F32, name="larger%d" % u) for u in range(2)]
         scores = []
         gates = []
 
@@ -106,7 +112,7 @@ def tile_attend_lenders_one_mixed_kernel(tc, query, keys_words, keys_scales, thr
             a = keep.tile([P, T], F32, name="a%d" % t)
             for n in range(T // BANK):
                 cols = slice(n * BANK, (n + 1) * BANK)
-                acc = psum_a.tile([P, BANK], F32, name="acc")
+                acc = psum.tile([P, BANK], F32, name="bank%d" % (2 * (t % 2) + n))
                 nc.tensor.matmul_mx(out=acc[:], lhsT=codes.bitcast(FP8X4), lhsT_scale=plane,
                                     rhs=key_words[:, 2 * n * BANK : 2 * (n + 1) * BANK].bitcast(FP4X4),
                                     rhs_scale=key_plane[:, cols], start=True, stop=True)
@@ -120,58 +126,93 @@ def tile_attend_lenders_one_mixed_kernel(tc, query, keys_words, keys_scales, thr
             nc.scalar.activation(out=s1, in_=a[:].indirect(offsets), func=ACT.Sigmoid,
                                  bias=thr_t[:, t : t + 1], scale=slope_t[:, t : t + 1])
 
-        def double(t, s1):
-            twice = keep.tile([P, I], F32, name="twice%d" % t)
-            nc.scalar.activation(out=twice[:], in_=s1[:], func=ACT.Copy, scale=2.0)
-            gates.append(twice)
+        def credit(s1, offsets):
+            nc.vector.tensor_tensor(out=lent_to[:].indirect(offsets), in0=s1, in1=s1, op=ALU.add)
 
-        def lend_first():
-            s1 = ring.tile([P, I], F32, name="s1")
-            for h in range(2):
-                half = s1[:, slots(h)]
-                gate(0, half, scores[0], gate_list[:, list_cols(h)])
-                nc.vector.tensor_tensor(out=lent_to[:].indirect(to_list[:, list_cols(h)]), in0=half, in1=half, op=ALU.add)
-            double(0, s1)
-            nc.vector.tensor_copy(out=lent_from[:].indirect(from_list[:]), in_=gates[0][:])
+        def debit(s1, factor, offsets):
+            nc.vector.tensor_tensor(out=lent_from[:].indirect(offsets), in0=s1, in1=factor, op=ALU.mult)
+
+        def open_gates(t):
+            s1 = keep.tile([P, I], F32, name="s1_%d" % t)
+            if t == 0:
+                for h in range(2):
+                    gate(t, s1[:, slots(h)], scores[t], gate_list[:, list_cols(h)])
+            else:
+                gate(t, s1[:], scores[t], gate_list[:])
+            gates.append(s1)
 
         def lend(t):
-            nc.vector.tensor_copy(out=lent_to[:].indirect(to_list[:]), in_=gates[t][:])
-            nc.vector.tensor_copy(out=lent_from[:].indirect(from_list[:]), in_=gates[t][:])
+            s1 = gates[t]
+            if t == 0:
+                for h in range(2):
+                    credit(s1[:, slots(h)], to_list[:, list_cols(h)])
+                    debit(s1[:, slots(h)], minus_two[:, slots(h)], from_list[:, list_cols(h)])
+            else:
+                credit(s1[:], to_list[:])
+                debit(s1[:], minus_two[:], from_list[:])
 
-        def doubled_gate(t):
-            s1 = ring.tile([P, I], F32, name="s1")
-            gate(t, s1[:], scores[t], gate_list[:])
-            double(t, s1)
+        def add_up(terms):
+            turned = ring.tile([P, T], F32, name="turned")
+            banks = [psum.tile([P, BANK], F32, name="bank%d" % n) for n in range(T // BANK)]
+            for k, term in enumerate(terms):
+                for c in range(T // P):
+                    n, b = divmod(c, BANK // P)
+                    nc.tensor.matmul(out=banks[n][:, b * P : (b + 1) * P], lhsT=term[:, c * P : (c + 1) * P], rhs=identity[:],
+                                     start=(k == 0 and b == 0), stop=(k == len(terms) - 1 and b == BANK // P - 1),
+                                     is_transpose=True)
+            sums = []
+            for n in range(T // BANK):
+                nc.scalar.copy(out=turned[:, n * BANK : (n + 1) * BANK], in_=banks[n][:])
+            for n in range(T // BANK):
+                back = psum.tile([P, BANK], F32, name="bank%d" % (2 + n))
+                for b in range(BANK // P):
+                    c = n * (BANK // P) + b
+                    nc.tensor.transpose(back[:, b * P : (b + 1) * P], turned[:, c * P : (c + 1) * P], identity[:])
+                sums.append(back)
+            return sums
 
-        def balance(t, engine):
-            part = ring.tile([P, T], F32, name="part")
-            nc.gpsimd.tensor_tensor(out=part[:], in0=scores[t][:], in1=lent_to[:], op=ALU.add)
+        def balance(t):
+            sums = add_up([scores[t], lent_to, lent_from])
             cc = ring.tile([P, T], F32, name="cc")
-            engine.tensor_tensor(out=cc[:], in0=part[:], in1=lent_from[:], op=ALU.subtract)
+            for n in range(T // BANK):
+                nc.scalar.copy(out=cc[:, n * BANK : (n + 1) * BANK], in_=sums[n][:])
             return cc
 
-        def weigh(t, h, larger):
-            nc.scalar.activation(out=gw[h][:, :, t], in_=larger, func=ACT.Copy, scale=rowf_t[:, t : t + 1])
+        def balance_last(t):
+            sums = add_up([scores[t], lent_to])
+            cc = ring.tile([P, T], F32, name="cc")
+            for n in range(T // BANK):
+                cols = slice(n * BANK, (n + 1) * BANK)
+                nc.vector.tensor_tensor(out=cc[:, cols], in0=sums[n][:], in1=lent_from[:, cols], op=ALU.add)
+            return cc
+
+        def weigh(t, cols, c4, c2):
+            g = larger[t // 2]
+            nc.vector.tensor_tensor(out=g[:, cols], in0=c4, in1=c2, op=ALU.max)
+            place = pairs[:, t // 2, cols, t % 2]
+            if t == PACK - 2:
+                nc.scalar.activation(out=place, in_=g[:, cols], func=ACT.Copy, scale=rowf_t[:, t : t + 1])
+            else:
+                nc.vector.tensor_scalar(out=place, in0=g[:, cols], scalar1=rowf_t[:, t : t + 1], scalar2=None, op0=ALU.mult)
 
         def pick(t, cc):
             c4 = ring.tile([P, I], F32, name="c4")
             c2 = ring.tile([P, I], F32, name="c2")
             nc.scalar.activation(out=c4[:], in_=cc[:].indirect(pick_list[:]), func=ACT.Copy)
             nc.scalar.activation(out=c2[:], in_=cc[:].indirect(to_list[:]), func=ACT.Copy)
-            nc.vector.tensor_tensor(out=g[:], in0=c4[:], in1=c2[:], op=ALU.max)
-            for h in range(2):
-                weigh(t, h, g[:, slots(h)])
+            weigh(t, slice(0, I), c4[:], c2[:])
 
         def pick_last(t, cc, h):
             c4 = ring.tile([P, HALF], F32, name="c4_last")
             c2 = ring.tile([P, HALF], F32, name="c2_last")
             nc.scalar.activation(out=c4[:], in_=cc[:].indirect(pick_list[:, list_cols(h)]), func=ACT.Copy)
             nc.vector.tensor_copy(out=c2[:], in_=cc[:].indirect(to_list[:, list_cols(h)]))
-            nc.vector.tensor_tensor(out=g[:, slots(h)], in0=c4[:], in1=c2[:], op=ALU.max)
-            if h == 0:
-                nc.vector.tensor_scalar(out=gw[h][:, :, t], in0=g[:, slots(h)], scalar1=rowf_t[:, t : t + 1], scalar2=None, op0=ALU.mult)
-            else:
-                weigh(t, h, g[:, slots(h)])
+            weigh(t, slots(h), c4[:], c2[:])
+
+        def weave(h):
+            words = gw[h][:].rearrange("p i t -> p (i t)").bitcast(U32).rearrange("p (i u) -> p i u", u=2)
+            nc.vector.tensor_copy(out=words,
+                                  in_=pairs_words[:, :, slots(h)].rearrange("p u i -> p i u"))
 
         def mix(h):
             codes = ring.tile([P, HALF], U32, name="gw_codes", align_bytes=64)
@@ -180,7 +221,7 @@ def tile_attend_lenders_one_mixed_kernel(tc, query, keys_words, keys_scales, thr
                                   in_=gw[h][:].rearrange("p i t -> p (i t)"))
             for e in range(E // P):
                 cols = slice(e * P, (e + 1) * P)
-                y = psum_y.tile([P, HALF], F32, name="y")
+                y = psum.tile([P, HALF], F32, name="y%d_%d" % (h, e))
                 nc.tensor.matmul_mx(out=y[:], lhsT=mix_codes[:, cols].bitcast(FP8X4), lhsT_scale=mix_plane[:, cols],
                                     rhs=codes[:].bitcast(FP8X4), rhs_scale=plane[:], start=True, stop=True)
                 y_out = keep.tile([P, HALF], F32, name="y_out%d_%d" % (h, e))
@@ -198,17 +239,19 @@ def tile_attend_lenders_one_mixed_kernel(tc, query, keys_words, keys_scales, thr
         quantise_queries(1, 2)
         deal_queries(3, 1)
         quantise_queries(3, 1)
-        lend_first()
+        open_gates(0)
+        lend(0)
         for t in range(1, PACK):
             score(t)
-            doubled_gate(t)
+            open_gates(t)
         last = PACK - 1
         for t in range(last):
-            cc = balance(t, nc.gpsimd)
+            cc = balance(t)
             lend(t + 1)
             pick(t, cc)
-        cc = balance(last, nc.vector)
+        cc_last = balance_last(last)
         for h in range(2):
-            pick_last(last, cc, h)
+            pick_last(last, cc_last, h)
         for h in range(2):
+            weave(h)
             mix(h)

@@ -32,6 +32,7 @@ def tile_attend_lenders_one_mixed_kernel(tc, query, keys_words, keys_scales, thr
         keep = ctx.enter_context(tc.tile_pool(name="keep", bufs=1))
         ring = ctx.enter_context(tc.tile_pool(name="ring", bufs=2))
         psum = ctx.enter_context(tc.psum_pool(name="psum", bufs=1))
+        banks = ctx.enter_context(tc.psum_pool(name="banks", bufs=3))
 
         def load_scale_rows(queue, plane, rows):
             for quad in range(4):
@@ -51,7 +52,9 @@ def tile_attend_lenders_one_mixed_kernel(tc, query, keys_words, keys_scales, thr
         key_plane = keep.tile([P, T], U8, align_bytes=64)
         nc.gpsimd.memset(key_plane[:].bitcast(I32), 0)
         q_raw = keep.tile([P, PACK, Q], F32)
-        nc.sync.dma_start(out=q_raw[:], in_=query.rearrange("(p j) q -> p j q", j=PACK))
+        q_rows = query.rearrange("(p j) q -> p j q", j=PACK)
+        for j in (0, 2):
+            nc.sync.dma_start(out=q_raw[:, j : j + 2], in_=q_rows[:, j : j + 2])
         load_scale_rows(nc.scalar, key_plane, keys_scales)
         key_words = keep.tile([P, 2 * T], U8, align_bytes=64)
         nc.sync.dma_start(out=key_words[:].bitcast(I32), in_=keys_words[0].bitcast(I32))
@@ -62,14 +65,15 @@ def tile_attend_lenders_one_mixed_kernel(tc, query, keys_words, keys_scales, thr
         from_list = load_list("from_list", offs3)
         pick_list = load_list("pick_list", offs4)
 
-        lent_to = keep.tile([P, T], F32)
+        lent_to = [keep.tile([P, T], F32, name="lent_to%d" % b) for b in range(2)]
         lent_from = keep.tile([P, T], F32)
-        nc.vector.memset(lent_to[:], 0.0)
+        nc.vector.memset(lent_to[0][:], 0.0)
         nc.vector.memset(lent_from[:], 0.0)
         minus_two = keep.tile([P, I], F32)
         nc.vector.memset(minus_two[:], -2.0)
         identity = keep.tile([P, P], F32)
         make_identity(nc, identity[:])
+        nc.gpsimd.memset(lent_to[1][:], 0.0)
 
         mix_plane = keep.tile([P, E], U8, align_bytes=64)
         nc.vector.memset(mix_plane[:].bitcast(I32), 0)
@@ -79,24 +83,22 @@ def tile_attend_lenders_one_mixed_kernel(tc, query, keys_words, keys_scales, thr
                           in_=mix_words[0].rearrange("p e r -> p (e r)").bitcast(I32))
         load_scale_rows(nc.sync, mix_plane, mix_scales)
 
-        q_bf16 = keep.tile([P, 2, P, PACK], BF16, align_bytes=64)
+        q_bf16 = keep.tile([P, PACK - 1, P, PACK], BF16, align_bytes=64)
         q_operands = []
 
-        def quantise_queries(t0, count):
-            codes = keep.tile([P, count * P], U32, name="q_codes%d" % t0, align_bytes=64)
-            plane = keep.tile([P, count * P], U8, name="q_plane%d" % t0, align_bytes=64)
+        def quantise_queries(t0, count, slot):
+            codes = keep.tile([P, count * P], U32, name="q_codes%d" % (t0 // 2), align_bytes=64)
+            plane = keep.tile([P, count * P], U8, name="q_plane%d" % (t0 % 2), align_bytes=64)
             nc.vector.quantize_mx(out=codes[:].bitcast(FP8X4), scales=plane[:],
-                                  in_=q_bf16[:, 0:count].rearrange("p t m j -> p (t m j)"))
+                                  in_=q_bf16[:, slot : slot + count].rearrange("p t m j -> p (t m j)"))
             for k in range(count):
                 q_operands.append((codes[:, k * P : (k + 1) * P], plane[:, k * P : (k + 1) * P]))
 
-        def deal_queries(t0, count):
-            nc.vector.tensor_copy(out=q_bf16[:, 0:count].rearrange("p t m j -> p m j t"),
-                                  in_=q_raw[:].rearrange("p j (m t) -> p m j t", t=PACK)[:, :, :, t0 : t0 + count])
+        def deal_queries(t0, count, rows):
+            nc.vector.tensor_copy(out=q_bf16[:, 0:count, :, rows].rearrange("p t m j -> p m j t"),
+                                  in_=q_raw[:, rows].rearrange("p j (m t) -> p m j t", t=PACK)[:, :, :, t0 : t0 + count])
 
         gw = [keep.tile([P, HALF, PACK], BF16, name="gw%d" % h, align_bytes=64) for h in range(2)]
-        pairs = keep.tile([P, 2, I, 2], BF16)
-        pairs_words = pairs[:].rearrange("p u i e -> p u (i e)").bitcast(U32)
         larger = [keep.tile([P, I], F32, name="larger%d" % u) for u in range(2)]
         scores = []
         gates = []
@@ -112,7 +114,7 @@ def tile_attend_lenders_one_mixed_kernel(tc, query, keys_words, keys_scales, thr
             a = keep.tile([P, T], F32, name="a%d" % t)
             for n in range(T // BANK):
                 cols = slice(n * BANK, (n + 1) * BANK)
-                acc = psum.tile([P, BANK], F32, name="bank%d" % (2 * (t % 2) + n))
+                acc = banks.tile([P, BANK], F32, name="bank")
                 nc.tensor.matmul_mx(out=acc[:], lhsT=codes.bitcast(FP8X4), lhsT_scale=plane,
                                     rhs=key_words[:, 2 * n * BANK : 2 * (n + 1) * BANK].bitcast(FP4X4),
                                     rhs_scale=key_plane[:, cols], start=True, stop=True)
@@ -126,8 +128,8 @@ def tile_attend_lenders_one_mixed_kernel(tc, query, keys_words, keys_scales, thr
             nc.scalar.activation(out=s1, in_=a[:].indirect(offsets), func=ACT.Sigmoid,
                                  bias=thr_t[:, t : t + 1], scale=slope_t[:, t : t + 1])
 
-        def credit(s1, offsets):
-            nc.vector.tensor_tensor(out=lent_to[:].indirect(offsets), in0=s1, in1=s1, op=ALU.add)
+        def credit(t, s1, offsets):
+            nc.vector.tensor_tensor(out=lent_to[min(t, 1)][:].indirect(offsets), in0=s1, in1=s1, op=ALU.add)
 
         def debit(s1, factor, offsets):
             nc.vector.tensor_tensor(out=lent_from[:].indirect(offsets), in0=s1, in1=factor, op=ALU.mult)
@@ -145,52 +147,52 @@ def tile_attend_lenders_one_mixed_kernel(tc, query, keys_words, keys_scales, thr
             s1 = gates[t]
             if t == 0:
                 for h in range(2):
-                    credit(s1[:, slots(h)], to_list[:, list_cols(h)])
+                    credit(t, s1[:, slots(h)], to_list[:, list_cols(h)])
                     debit(s1[:, slots(h)], minus_two[:, slots(h)], from_list[:, list_cols(h)])
             else:
-                credit(s1[:], to_list[:])
+                credit(t, s1[:], to_list[:])
                 debit(s1[:], minus_two[:], from_list[:])
 
         def add_up(terms):
             turned = ring.tile([P, T], F32, name="turned")
-            banks = [psum.tile([P, BANK], F32, name="bank%d" % n) for n in range(T // BANK)]
+            per_bank = BANK // P
+            summed = [banks.tile([P, BANK], F32, name="bank") for n in range(T // BANK)]
             for k, term in enumerate(terms):
                 for c in range(T // P):
-                    n, b = divmod(c, BANK // P)
-                    nc.tensor.matmul(out=banks[n][:, b * P : (b + 1) * P], lhsT=term[:, c * P : (c + 1) * P], rhs=identity[:],
-                                     start=(k == 0 and b == 0), stop=(k == len(terms) - 1 and b == BANK // P - 1),
+                    n, b = divmod(c, per_bank)
+                    nc.tensor.matmul(out=summed[n][:, b * P : (b + 1) * P], lhsT=term[:, c * P : (c + 1) * P], rhs=identity[:],
+                                     start=(k == 0 and b == 0), stop=(k == len(terms) - 1 and b == per_bank - 1),
                                      is_transpose=True)
-            sums = []
             for n in range(T // BANK):
-                nc.scalar.copy(out=turned[:, n * BANK : (n + 1) * BANK], in_=banks[n][:])
-            for n in range(T // BANK):
-                back = psum.tile([P, BANK], F32, name="bank%d" % (2 + n))
-                for b in range(BANK // P):
-                    c = n * (BANK // P) + b
-                    nc.tensor.transpose(back[:, b * P : (b + 1) * P], turned[:, c * P : (c + 1) * P], identity[:])
-                sums.append(back)
-            return sums
+                nc.scalar.copy(out=turned[:, n * BANK : (n + 1) * BANK], in_=summed[n][:])
+            back = [banks.tile([P, BANK], F32, name="bank") for n in range(T // BANK)]
+            for c in range(T // P):
+                n, b = divmod(c, per_bank)
+                nc.tensor.transpose(back[n][:, b * P : (b + 1) * P], turned[:, c * P : (c + 1) * P], identity[:])
+            return back
 
         def balance(t):
-            sums = add_up([scores[t], lent_to, lent_from])
-            cc = ring.tile([P, T], F32, name="cc")
+            back = add_up([scores[t], lent_to[min(t, 1)], lent_from])
+            cc = keep.tile([P, T], F32, name="cc%d" % t)
             for n in range(T // BANK):
-                nc.scalar.copy(out=cc[:, n * BANK : (n + 1) * BANK], in_=sums[n][:])
+                nc.scalar.copy(out=cc[:, n * BANK : (n + 1) * BANK], in_=back[n][:])
             return cc
 
         def balance_last(t):
-            sums = add_up([scores[t], lent_to])
-            cc = ring.tile([P, T], F32, name="cc")
+            back = add_up([scores[t], lent_to[min(t, 1)]])
+            cc = keep.tile([P, T], F32, name="cc%d" % t)
             for n in range(T // BANK):
                 cols = slice(n * BANK, (n + 1) * BANK)
-                nc.vector.tensor_tensor(out=cc[:, cols], in0=sums[n][:], in1=lent_from[:, cols], op=ALU.add)
+                nc.vector.tensor_tensor(out=cc[:, cols], in0=back[n][:], in1=lent_from[:, cols], op=ALU.add)
             return cc
 
-        def weigh(t, cols, c4, c2):
+        def take_larger(t, cols, c4, c2):
+            nc.vector.tensor_tensor(out=larger[t // 2][:, cols], in0=c4, in1=c2, op=ALU.max)
+
+        def weigh(t, cols, pairs):
             g = larger[t // 2]
-            nc.vector.tensor_tensor(out=g[:, cols], in0=c4, in1=c2, op=ALU.max)
             place = pairs[:, t // 2, cols, t % 2]
-            if t == PACK - 2:
+            if t % 2 == 0:
                 nc.scalar.activation(out=place, in_=g[:, cols], func=ACT.Copy, scale=rowf_t[:, t : t + 1])
             else:
                 nc.vector.tensor_scalar(out=place, in0=g[:, cols], scalar1=rowf_t[:, t : t + 1], scalar2=None, op0=ALU.mult)
@@ -200,16 +202,18 @@ def tile_attend_lenders_one_mixed_kernel(tc, query, keys_words, keys_scales, thr
             c2 = ring.tile([P, I], F32, name="c2")
             nc.scalar.activation(out=c4[:], in_=cc[:].indirect(pick_list[:]), func=ACT.Copy)
             nc.scalar.activation(out=c2[:], in_=cc[:].indirect(to_list[:]), func=ACT.Copy)
-            weigh(t, slice(0, I), c4[:], c2[:])
+            return c4, c2
 
-        def pick_last(t, cc, h):
+        def pick_last(t, cc, h, pairs):
             c4 = ring.tile([P, HALF], F32, name="c4_last")
             c2 = ring.tile([P, HALF], F32, name="c2_last")
             nc.scalar.activation(out=c4[:], in_=cc[:].indirect(pick_list[:, list_cols(h)]), func=ACT.Copy)
             nc.vector.tensor_copy(out=c2[:], in_=cc[:].indirect(to_list[:, list_cols(h)]))
-            weigh(t, slots(h), c4[:], c2[:])
+            take_larger(t, slots(h), c4[:], c2[:])
+            weigh(t, slots(h), pairs)
 
-        def weave(h):
+        def weave(h, pairs):
+            pairs_words = pairs[:].rearrange("p u i e -> p u (i e)").bitcast(U32)
             words = gw[h][:].rearrange("p i t -> p (i t)").bitcast(U32).rearrange("p (i u) -> p i u", u=2)
             nc.vector.tensor_copy(out=words,
                                   in_=pairs_words[:, :, slots(h)].rearrange("p u i -> p i u"))
@@ -232,26 +236,33 @@ def tile_attend_lenders_one_mixed_kernel(tc, query, keys_words, keys_scales, thr
                     nc.scalar.copy(out=y_out[:], in_=y[:])
                     nc.scalar.dma_start(out=out[cols, slots(h)], in_=y_out[:])
 
-        deal_queries(0, 1)
-        quantise_queries(0, 1)
-        deal_queries(1, 2)
+        for j in (0, 2):
+            deal_queries(0, 1, slice(j, j + 2))
+        quantise_queries(0, 1, 0)
+        deal_queries(1, 3, slice(0, PACK))
         score(0)
-        quantise_queries(1, 2)
-        deal_queries(3, 1)
-        quantise_queries(3, 1)
+        quantise_queries(1, 1, 0)
+        quantise_queries(2, 2, 1)
         open_gates(0)
         lend(0)
         for t in range(1, PACK):
             score(t)
             open_gates(t)
         last = PACK - 1
+        every = slice(0, I)
         for t in range(last):
             cc = balance(t)
             lend(t + 1)
-            pick(t, cc)
+            c4, c2 = pick(t, cc)
+            if t == 1:
+                pairs = keep.tile([P, 2, I, 2], BF16, name="cc1")
+                weigh(0, every, pairs)
+            take_larger(t, every, c4[:], c2[:])
+            if t > 0:
+                weigh(t, every, pairs)
         cc_last = balance_last(last)
         for h in range(2):
-            pick_last(last, cc_last, h)
+            pick_last(last, cc_last, h, pairs)
         for h in range(2):
-            weave(h)
+            weave(h, pairs)
             mix(h)

@@ -20,6 +20,7 @@ ACT = mybir.ActivationFunctionType
 P = 128
 PACK = 4
 BANK = 512
+PIECE = 256
 HALF = I // 2
 LIST_COLS = I // 16
 
@@ -32,7 +33,7 @@ def tile_attend_lenders_one_mixed_kernel(tc, query, keys_words, keys_scales, thr
         keep = ctx.enter_context(tc.tile_pool(name="keep", bufs=1))
         ring = ctx.enter_context(tc.tile_pool(name="ring", bufs=2))
         psum = ctx.enter_context(tc.psum_pool(name="psum", bufs=1))
-        banks = ctx.enter_context(tc.psum_pool(name="banks", bufs=3))
+        banks = ctx.enter_context(tc.psum_pool(name="banks", bufs=5))
 
         def load_scale_rows(queue, plane, rows):
             for quad in range(4):
@@ -67,13 +68,12 @@ def tile_attend_lenders_one_mixed_kernel(tc, query, keys_words, keys_scales, thr
 
         lent_to = [keep.tile([P, T], F32, name="lent_to%d" % b) for b in range(2)]
         lent_from = keep.tile([P, T], F32)
-        nc.vector.memset(lent_to[0][:], 0.0)
-        nc.vector.memset(lent_from[:], 0.0)
+        for window in lent_to + [lent_from]:
+            nc.vector.memset(window[:], 0.0)
         minus_two = keep.tile([P, I], F32)
         nc.vector.memset(minus_two[:], -2.0)
         identity = keep.tile([P, P], F32)
         make_identity(nc, identity[:])
-        nc.gpsimd.memset(lent_to[1][:], 0.0)
 
         mix_plane = keep.tile([P, E], U8, align_bytes=64)
         nc.vector.memset(mix_plane[:].bitcast(I32), 0)
@@ -153,36 +153,35 @@ def tile_attend_lenders_one_mixed_kernel(tc, query, keys_words, keys_scales, thr
                 credit(t, s1[:], to_list[:])
                 debit(s1[:], minus_two[:], from_list[:])
 
-        def add_up(terms):
-            turned = ring.tile([P, T], F32, name="turned")
-            per_bank = BANK // P
-            summed = [banks.tile([P, BANK], F32, name="bank") for n in range(T // BANK)]
+        def add_up(t, terms):
+            turned = keep.tile([P, T], F32, name="wide%d" % (t % 2))
+            per_piece = PIECE // P
+            summed = [banks.tile([P, PIECE], F32, name="bank") for n in range(T // PIECE)]
             for k, term in enumerate(terms):
                 for c in range(T // P):
-                    n, b = divmod(c, per_bank)
+                    n, b = divmod(c, per_piece)
                     nc.tensor.matmul(out=summed[n][:, b * P : (b + 1) * P], lhsT=term[:, c * P : (c + 1) * P], rhs=identity[:],
-                                     start=(k == 0 and b == 0), stop=(k == len(terms) - 1 and b == per_bank - 1),
+                                     start=(k == 0 and b == 0), stop=(k == len(terms) - 1 and b == per_piece - 1),
                                      is_transpose=True)
-            for n in range(T // BANK):
-                nc.scalar.copy(out=turned[:, n * BANK : (n + 1) * BANK], in_=summed[n][:])
-            back = [banks.tile([P, BANK], F32, name="bank") for n in range(T // BANK)]
+            for n in range(T // PIECE):
+                nc.scalar.copy(out=turned[:, n * PIECE : (n + 1) * PIECE], in_=summed[n][:])
+            back = [banks.tile([P, PIECE], F32, name="bank") for n in range(T // PIECE)]
             for c in range(T // P):
-                n, b = divmod(c, per_bank)
+                n, b = divmod(c, per_piece)
                 nc.tensor.transpose(back[n][:, b * P : (b + 1) * P], turned[:, c * P : (c + 1) * P], identity[:])
             return back
 
         def balance(t):
-            back = add_up([scores[t], lent_to[min(t, 1)], lent_from])
-            cc = keep.tile([P, T], F32, name="cc%d" % t)
-            for n in range(T // BANK):
-                nc.scalar.copy(out=cc[:, n * BANK : (n + 1) * BANK], in_=back[n][:])
+            back = add_up(t, [scores[t], lent_to[0], lent_from] if t == 0 else [lent_to[1], scores[t], lent_from])
+            cc = keep.tile([P, T], F32, name="wide%d" % ((t + 1) % 2))
+            for n in range(T // PIECE):
+                nc.scalar.copy(out=cc[:, n * PIECE : (n + 1) * PIECE], in_=back[n][:])
             return cc
 
-        def balance_last(t):
-            back = add_up([scores[t], lent_to[min(t, 1)]])
-            cc = keep.tile([P, T], F32, name="cc%d" % t)
-            for n in range(T // BANK):
-                cols = slice(n * BANK, (n + 1) * BANK)
+        def balance_last(t, back):
+            cc = keep.tile([P, T], F32, name="wide%d" % ((t + 1) % 2))
+            for n in range(T // PIECE):
+                cols = slice(n * PIECE, (n + 1) * PIECE)
                 nc.vector.tensor_tensor(out=cc[:, cols], in0=back[n][:], in1=lent_from[:, cols], op=ALU.add)
             return cc
 
@@ -192,7 +191,7 @@ def tile_attend_lenders_one_mixed_kernel(tc, query, keys_words, keys_scales, thr
         def weigh(t, cols, pairs):
             g = larger[t // 2]
             place = pairs[:, t // 2, cols, t % 2]
-            if t % 2 == 0:
+            if t == 2:
                 nc.scalar.activation(out=place, in_=g[:, cols], func=ACT.Copy, scale=rowf_t[:, t : t + 1])
             else:
                 nc.vector.tensor_scalar(out=place, in0=g[:, cols], scalar1=rowf_t[:, t : t + 1], scalar2=None, op0=ALU.mult)
@@ -225,7 +224,7 @@ def tile_attend_lenders_one_mixed_kernel(tc, query, keys_words, keys_scales, thr
                                   in_=gw[h][:].rearrange("p i t -> p (i t)"))
             for e in range(E // P):
                 cols = slice(e * P, (e + 1) * P)
-                y = psum.tile([P, HALF], F32, name="y%d_%d" % (h, e))
+                y = psum.tile([P, HALF], F32, name="y%d" % e) if h == 0 else banks.tile([P, HALF], F32, name="bank")
                 nc.tensor.matmul_mx(out=y[:], lhsT=mix_codes[:, cols].bitcast(FP8X4), lhsT_scale=mix_plane[:, cols],
                                     rhs=codes[:].bitcast(FP8X4), rhs_scale=plane[:], start=True, stop=True)
                 y_out = keep.tile([P, HALF], F32, name="y_out%d_%d" % (h, e))
@@ -245,8 +244,11 @@ def tile_attend_lenders_one_mixed_kernel(tc, query, keys_words, keys_scales, thr
         quantise_queries(2, 2, 1)
         open_gates(0)
         lend(0)
-        for t in range(1, PACK):
+        score(1)
+        open_gates(1)
+        for t in range(2, PACK):
             score(t)
+        for t in range(2, PACK):
             open_gates(t)
         last = PACK - 1
         every = slice(0, I)
@@ -255,12 +257,14 @@ def tile_attend_lenders_one_mixed_kernel(tc, query, keys_words, keys_scales, thr
             lend(t + 1)
             c4, c2 = pick(t, cc)
             if t == 1:
-                pairs = keep.tile([P, 2, I, 2], BF16, name="cc1")
+                pairs = keep.tile([P, 2, I, 2], BF16, name="pairs")
                 weigh(0, every, pairs)
+            if t == last - 1:
+                credited = add_up(last, [lent_to[1], scores[last]])
             take_larger(t, every, c4[:], c2[:])
             if t > 0:
                 weigh(t, every, pairs)
-        cc_last = balance_last(last)
+        cc_last = balance_last(last, credited)
         for h in range(2):
             pick_last(last, cc_last, h, pairs)
         for h in range(2):

from contextlib import ExitStack

import concourse.mybir as mybir
from concourse.masks import make_identity

D, T, I, Q, E = 512, 1024, 512, 512, 256
FLOPS = 2 * D * Q * T + 2 * Q * E * I

F32 = mybir.dt.float32
BF16 = mybir.dt.bfloat16
I32 = mybir.dt.int32
U32 = mybir.dt.uint32
U16 = mybir.dt.uint16
U8 = mybir.dt.uint8
FP8X4 = mybir.dt.float8_e4m3fn_x4
FP4X4 = mybir.dt.float4_e2m1fn_x4
ALU = mybir.AluOpType
ACT = mybir.ActivationFunctionType

P = 128
PACK = 4
BANK = 512
PIECE = 256
HALF = I // 2
LIST_COLS = I // 16


def tile_attend_lenders_one_mixed_kernel(tc, query, keys_words, keys_scales, thr, slope, rowf,
                                          mix_words, mix_scales, offs, offs2, offs3, offs4, out):
    nc = tc.nc
    with ExitStack() as ctx:
        lists = ctx.enter_context(tc.tile_pool(name="lists", bufs=1))
        keep = ctx.enter_context(tc.tile_pool(name="keep", bufs=1))
        ring = ctx.enter_context(tc.tile_pool(name="ring", bufs=2))
        psum = ctx.enter_context(tc.psum_pool(name="psum", bufs=1))
        banks = ctx.enter_context(tc.psum_pool(name="banks", bufs=5))

        def load_scale_rows(queue, plane, rows):
            for quad in range(4):
                queue.dma_start(out=plane[32 * quad : 32 * quad + 4, :].bitcast(I32),
                                in_=rows[0, 4 * quad : 4 * quad + 4, :].bitcast(I32))

        def load_list(name, source):
            tile = lists.tile([P, LIST_COLS], U16, name=name)
            nc.sync.dma_start(tile[:], source)
            return tile

        def load_row_values(queue, name, source):
            tile = keep.tile([P, PACK], F32, name=name)
            queue.dma_start(out=tile[:], in_=source.rearrange("(p t) o -> p (t o)", t=PACK))
            return tile

        key_plane = keep.tile([P, T], U8, align_bytes=64)
        nc.gpsimd.memset(key_plane[:].bitcast(I32), 0)
        q_raw = keep.tile([P, PACK, Q], F32)
        q_rows = query.rearrange("(p j) q -> p j q", j=PACK)
        for j in (0, 2):
            nc.sync.dma_start(out=q_raw[:, j : j + 2], in_=q_rows[:, j : j + 2])
        load_scale_rows(nc.scalar, key_plane, keys_scales)
        key_words = keep.tile([P, 2 * T], U8, align_bytes=64)
        nc.sync.dma_start(out=key_words[:].bitcast(I32), in_=keys_words[0].bitcast(I32))
        slope_t = load_row_values(nc.gpsimd, "slope_t", slope)
        thr_t = load_row_values(nc.gpsimd, "thr_t", thr)
        gate_list = load_list("gate_list", offs)
        to_list = load_list("to_list", offs2)
        from_list = load_list("from_list", offs3)
        pick_list = load_list("pick_list", offs4)

        lent_to = [keep.tile([P, T], F32, name="lent_to%d" % b) for b in range(2)]
        lent_from = keep.tile([P, T], F32)
        for window in lent_to + [lent_from]:
            nc.vector.memset(window[:], 0.0)
        minus_two = keep.tile([P, I], F32)
        nc.vector.memset(minus_two[:], -2.0)
        identity = keep.tile([P, P], F32)
        make_identity(nc, identity[:])

        mix_plane = keep.tile([P, E], U8, align_bytes=64)
        nc.vector.memset(mix_plane[:].bitcast(I32), 0)
        rowf_t = load_row_values(nc.sync, "rowf_t", rowf)
        mix_codes = keep.tile([P, E], U32, align_bytes=64)
        nc.sync.dma_start(out=mix_codes[:].bitcast(I32),
                          in_=mix_words[0].rearrange("p e r -> p (e r)").bitcast(I32))
        load_scale_rows(nc.sync, mix_plane, mix_scales)

        q_bf16 = keep.tile([P, PACK - 1, P, PACK], BF16, align_bytes=64)
        q_operands = []

        def quantise_queries(t0, count, slot):
            codes = keep.tile([P, count * P], U32, name="q_codes%d" % (t0 // 2), align_bytes=64)
            plane = keep.tile([P, count * P], U8, name="q_plane%d" % (t0 % 2), align_bytes=64)
            nc.vector.quantize_mx(out=codes[:].bitcast(FP8X4), scales=plane[:],
                                  in_=q_bf16[:, slot : slot + count].rearrange("p t m j -> p (t m j)"))
            for k in range(count):
                q_operands.append((codes[:, k * P : (k + 1) * P], plane[:, k * P : (k + 1) * P]))

        def deal_queries(t0, count, rows):
            nc.vector.tensor_copy(out=q_bf16[:, 0:count, :, rows].rearrange("p t m j -> p m j t"),
                                  in_=q_raw[:, rows].rearrange("p j (m t) -> p m j t", t=PACK)[:, :, :, t0 : t0 + count])

        gw = [keep.tile([P, HALF, PACK], BF16, name="gw%d" % h, align_bytes=64) for h in range(2)]
        larger = [keep.tile([P, I], F32, name="larger%d" % u) for u in range(2)]
        scores = []
        gates = []

        def slots(h):
            return slice(h * HALF, (h + 1) * HALF)

        def list_cols(h):
            return slice(h * LIST_COLS // 2, (h + 1) * LIST_COLS // 2)

        def score(t):
            codes, plane = q_operands[t]
            a = keep.tile([P, T], F32, name="a%d" % t)
            for n in range(T // BANK):
                cols = slice(n * BANK, (n + 1) * BANK)
                acc = banks.tile([P, BANK], F32, name="bank")
                nc.tensor.matmul_mx(out=acc[:], lhsT=codes.bitcast(FP8X4), lhsT_scale=plane,
                                    rhs=key_words[:, 2 * n * BANK : 2 * (n + 1) * BANK].bitcast(FP4X4),
                                    rhs_scale=key_plane[:, cols], start=True, stop=True)
                if t == 0:
                    nc.vector.tensor_copy(out=a[:, cols], in_=acc[:])
                else:
                    nc.scalar.copy(out=a[:, cols], in_=acc[:])
            scores.append(a)

        def gate(t, s1, a, offsets):
            nc.scalar.activation(out=s1, in_=a[:].indirect(offsets), func=ACT.Sigmoid,
                                 bias=thr_t[:, t : t + 1], scale=slope_t[:, t : t + 1])

        def credit(t, s1, offsets):
            nc.vector.tensor_tensor(out=lent_to[min(t, 1)][:].indirect(offsets), in0=s1, in1=s1, op=ALU.add)

        def debit(s1, factor, offsets):
            nc.vector.tensor_tensor(out=lent_from[:].indirect(offsets), in0=s1, in1=factor, op=ALU.mult)

        def open_gates(t):
            s1 = keep.tile([P, I], F32, name="s1_%d" % t)
            if t == 0:
                for h in range(2):
                    gate(t, s1[:, slots(h)], scores[t], gate_list[:, list_cols(h)])
            else:
                gate(t, s1[:], scores[t], gate_list[:])
            gates.append(s1)

        def lend(t):
            s1 = gates[t]
            if t == 0:
                for h in range(2):
                    credit(t, s1[:, slots(h)], to_list[:, list_cols(h)])
                    debit(s1[:, slots(h)], minus_two[:, slots(h)], from_list[:, list_cols(h)])
            else:
                credit(t, s1[:], to_list[:])
                debit(s1[:], minus_two[:], from_list[:])

        def add_up(t, terms):
            turned = keep.tile([P, T], F32, name="wide%d" % (t % 2))
            per_piece = PIECE // P
            summed = [banks.tile([P, PIECE], F32, name="bank") for n in range(T // PIECE)]
            for k, term in enumerate(terms):
                for c in range(T // P):
                    n, b = divmod(c, per_piece)
                    nc.tensor.matmul(out=summed[n][:, b * P : (b + 1) * P], lhsT=term[:, c * P : (c + 1) * P], rhs=identity[:],
                                     start=(k == 0 and b == 0), stop=(k == len(terms) - 1 and b == per_piece - 1),
                                     is_transpose=True)
            for n in range(T // PIECE):
                nc.scalar.copy(out=turned[:, n * PIECE : (n + 1) * PIECE], in_=summed[n][:])
            back = [banks.tile([P, PIECE], F32, name="bank") for n in range(T // PIECE)]
            for c in range(T // P):
                n, b = divmod(c, per_piece)
                nc.tensor.transpose(back[n][:, b * P : (b + 1) * P], turned[:, c * P : (c + 1) * P], identity[:])
            return back

        def balance(t):
            back = add_up(t, [scores[t], lent_to[0], lent_from] if t == 0 else [lent_to[1], scores[t], lent_from])
            cc = keep.tile([P, T], F32, name="wide%d" % ((t + 1) % 2))
            for n in range(T // PIECE):
                nc.scalar.copy(out=cc[:, n * PIECE : (n + 1) * PIECE], in_=back[n][:])
            return cc

        def balance_last(t, back):
            cc = keep.tile([P, T], F32, name="wide%d" % ((t + 1) % 2))
            for n in range(T // PIECE):
                cols = slice(n * PIECE, (n + 1) * PIECE)
                nc.vector.tensor_tensor(out=cc[:, cols], in0=back[n][:], in1=lent_from[:, cols], op=ALU.add)
            return cc

        def take_larger(t, cols, c4, c2):
            nc.vector.tensor_tensor(out=larger[t // 2][:, cols], in0=c4, in1=c2, op=ALU.max)

        def weigh(t, cols, pairs):
            g = larger[t // 2]
            place = pairs[:, t // 2, cols, t % 2]
            if t == 2:
                nc.scalar.activation(out=place, in_=g[:, cols], func=ACT.Copy, scale=rowf_t[:, t : t + 1])
            else:
                nc.vector.tensor_scalar(out=place, in0=g[:, cols], scalar1=rowf_t[:, t : t + 1], scalar2=None, op0=ALU.mult)

        def pick(t, cc):
            c4 = ring.tile([P, I], F32, name="c4")
            c2 = ring.tile([P, I], F32, name="c2")
            nc.scalar.activation(out=c4[:], in_=cc[:].indirect(pick_list[:]), func=ACT.Copy)
            nc.scalar.activation(out=c2[:], in_=cc[:].indirect(to_list[:]), func=ACT.Copy)
            return c4, c2

        def pick_last(t, cc, h, pairs):
            c4 = ring.tile([P, HALF], F32, name="c4_last")
            c2 = ring.tile([P, HALF], F32, name="c2_last")
            nc.scalar.activation(out=c4[:], in_=cc[:].indirect(pick_list[:, list_cols(h)]), func=ACT.Copy)
            nc.vector.tensor_copy(out=c2[:], in_=cc[:].indirect(to_list[:, list_cols(h)]))
            take_larger(t, slots(h), c4[:], c2[:])
            weigh(t, slots(h), pairs)

        def weave(h, pairs):
            pairs_words = pairs[:].rearrange("p u i e -> p u (i e)").bitcast(U32)
            words = gw[h][:].rearrange("p i t -> p (i t)").bitcast(U32).rearrange("p (i u) -> p i u", u=2)
            nc.vector.tensor_copy(out=words,
                                  in_=pairs_words[:, :, slots(h)].rearrange("p u i -> p i u"))

        def mix(h):
            codes = ring.tile([P, HALF], U32, name="gw_codes", align_bytes=64)
            plane = ring.tile([P, HALF], U8, name="gw_plane", align_bytes=64)
            nc.vector.quantize_mx(out=codes[:].bitcast(FP8X4), scales=plane[:],
                                  in_=gw[h][:].rearrange("p i t -> p (i t)"))
            for e in range(E // P):
                cols = slice(e * P, (e + 1) * P)
                y = psum.tile([P, HALF], F32, name="y%d" % e) if h == 0 else banks.tile([P, HALF], F32, name="bank")
                nc.tensor.matmul_mx(out=y[:], lhsT=mix_codes[:, cols].bitcast(FP8X4), lhsT_scale=mix_plane[:, cols],
                                    rhs=codes[:].bitcast(FP8X4), rhs_scale=plane[:], start=True, stop=True)
                y_out = keep.tile([P, HALF], F32, name="y_out%d_%d" % (h, e))
                if e == 0:
                    nc.vector.tensor_copy(out=y_out[:], in_=y[:])
                    nc.sync.dma_start(out=out[cols, slots(h)], in_=y_out[:])
                else:
                    nc.scalar.copy(out=y_out[:], in_=y[:])
                    nc.scalar.dma_start(out=out[cols, slots(h)], in_=y_out[:])

        for j in (0, 2):
            deal_queries(0, 1, slice(j, j + 2))
        quantise_queries(0, 1, 0)
        deal_queries(1, 3, slice(0, PACK))
        score(0)
        quantise_queries(1, 1, 0)
        quantise_queries(2, 2, 1)
        open_gates(0)
        lend(0)
        score(1)
        open_gates(1)
        for t in range(2, PACK):
            score(t)
        for t in range(2, PACK):
            open_gates(t)
        last = PACK - 1
        every = slice(0, I)
        for t in range(last):
            cc = balance(t)
            lend(t + 1)
            c4, c2 = pick(t, cc)
            if t == 1:
                pairs = keep.tile([P, 2, I, 2], BF16, name="pairs")
                weigh(0, every, pairs)
            if t == last - 1:
                credited = add_up(last, [lent_to[1], scores[last]])
            take_larger(t, every, c4[:], c2[:])
            if t > 0:
                weigh(t, every, pairs)
        cc_last = balance_last(last, credited)
        for h in range(2):
            pick_last(last, cc_last, h, pairs)
        for h in range(2):
            weave(h, pairs)
            mix(h)
